import numpy as np
import ml_dtypes


def mxq(x, axis, fmt="e4m3"):
    dtype, down = {"e4m3": (ml_dtypes.float8_e4m3fn, 7), "e5m2": (ml_dtypes.float8_e5m2, 14)}[fmt]
    v = np.moveaxis(np.asarray(x, np.float32).astype(ml_dtypes.bfloat16).astype(np.float64), axis, -1)
    blocks = v.reshape(v.shape[:-1] + (-1, 32))
    amax = np.abs(blocks).max(-1, keepdims=True)
    byte = np.maximum(np.where(amax > 0, np.frexp(amax)[1] - 1 + 127, 0) - down, 1)
    scale = np.exp2(byte - 127.0)
    codes = (blocks / scale).astype(np.float32).astype(dtype).astype(np.float64)
    return np.moveaxis((codes * scale).reshape(v.shape), -1, axis)


WIDE = False


def mx_kscale(k):
    if not WIDE:
        return np.ones(k)
    levels = np.array([10, -10, 5, -5, 0])
    if k % 512:
        return np.exp2(np.random.permutation(np.resize(levels, k // 32))).repeat(32)
    a = np.empty((k // 512, 16))
    for p in range(k // 512):
        a[p, :8] = np.random.permutation(np.resize(levels, 8))
        for g in range(8):
            far = levels[np.abs(levels - a[p, g]) >= 10]
            a[p, g + 8] = far[np.random.randint(len(far))]
    return np.exp2(a.ravel()).repeat(32)


BF16 = ml_dtypes.bfloat16


def bf(x):
    return np.asarray(x, np.float32).astype(BF16)


def f64(x):
    return np.asarray(x).astype(np.float64)


E2M1 = np.array([0.0, 0.5, 1.0, 1.5, 2.0, 3.0, 4.0, 6.0, -0.0, -0.5, -1.0, -1.5, -2.0, -3.0, -4.0, -6.0])


def pack_weight(w, fmt):
    k, n = w.shape
    w = f64(bf(w)).reshape(k // 32, 32, n)
    amax = np.abs(w).max(1)
    if fmt == "e4m3":
        byte = np.frexp(amax)[1] - 1 + 127 - 7
    else:
        mant, ex = np.frexp(amax / 6.0)
        byte = np.where(mant > 0.5, ex, ex - 1) + 127
    byte = np.clip(np.where(amax > 0, byte, 1), 1, 254)
    scaled = (w * np.exp2(127.0 - byte)[:, None, :]).reshape(k, n).astype(np.float32)
    by_word = np.ascontiguousarray(scaled.reshape(k // 512, 128, 4, n).transpose(0, 1, 3, 2))
    if fmt == "e4m3":
        words = by_word.astype(ml_dtypes.float8_e4m3fn).view(np.uint8)
    else:
        c = by_word.astype(ml_dtypes.float4_e2m1fn).view(np.uint8) & 0xF
        words = c[..., 0::2] | (c[..., 1::2] << 4)
    return np.ascontiguousarray(words), np.ascontiguousarray(byte.astype(np.uint8).reshape(k // 512, 16, n))


def unpack_weight(words, scales, fmt):
    g, p, n, _ = words.shape
    if fmt == "e4m3":
        vals = np.ascontiguousarray(words).view(ml_dtypes.float8_e4m3fn).astype(np.float64)
    else:
        nib = np.empty((g, p, n, 4), np.uint8)
        nib[..., 0::2] = words & 0xF
        nib[..., 1::2] = words >> 4
        vals = E2M1[nib]
    vals = vals * np.repeat(np.exp2(scales.astype(np.float64) - 127.0), 8, axis=1)[..., None]
    return vals.transpose(0, 1, 3, 2).reshape(g * 512, n)
def pack4(w):
    words, scales = pack_weight(w, "e2m1")
    return words.reshape(words.shape[0], 128, -1), scales


def unpack4(words, scales):
    return unpack_weight(words.reshape(words.shape[0], 128, -1, 2), scales, "e2m1")


B, S, K, F, D = 256, 8, 1024, 1024, 2048


def setup_inputs():
    s, t = mx_kscale(K), mx_kscale(F)
    xt = np.random.standard_normal((K, B * S)) * s[:, None]
    wv = np.random.standard_normal((K, F)) / np.sqrt(K) / s[:, None] * t
    wa = np.random.standard_normal((K, F)) / np.sqrt(K) / s[:, None]
    wo = np.random.standard_normal((F, D)) / np.sqrt(F) / t[:, None]
    x_words, x_scales = pack4(xt)
    wv_words, wv_scales = pack4(wv)
    wa_words, wa_scales = pack4(wa)
    wo_words, wo_scales = pack4(wo)
    return {"x_words": x_words, "x_scales": x_scales,
            "wv_words": wv_words, "wv_scales": wv_scales,
            "wa_words": wa_words, "wa_scales": wa_scales,
            "b": bf(0.3 * np.random.standard_normal(F) * t),
            "prior": bf(0.5 * np.random.standard_normal((B, S))),
            "wo_words": wo_words, "wo_scales": wo_scales,
            "c": bf(0.3 * np.random.standard_normal(D)),
            "gain": bf(1 + 0.1 * np.random.standard_normal(D))}


def reference(x_words, x_scales, wv_words, wv_scales, wa_words, wa_scales, b, prior, wo_words, wo_scales, c, gain):
    xt = unpack4(x_words, x_scales)
    wv = unpack4(wv_words, wv_scales)
    wa = unpack4(wa_words, wa_scales)
    wo = unpack4(wo_words, wo_scales)
    v = xt.T @ wv
    a = xt.T @ wa
    h = np.maximum(v + f64(b), 0.0).reshape(B, S, F)
    l = a.reshape(B, S, F) + f64(prior)[:, :, None]
    e = np.exp(l - np.max(l, axis=1, keepdims=True))
    p = e / np.sum(e, axis=1, keepdims=True)
    pooled = np.sum(p * h, axis=1)
    y = (mxq(pooled, 1, "e4m3") @ wo) + f64(c)
    return y / np.sqrt(np.mean(y * y, axis=1, keepdims=True)) * f64(gain)

@@ -1,0 +1,465 @@
+from contextlib import ExitStack
+
+import concourse.mybir as mybir
+from concourse.masks import make_identity
+
+F32 = mybir.dt.float32
+BF16 = mybir.dt.bfloat16
+U32 = mybir.dt.uint32
+I32 = mybir.dt.int32
+U8 = mybir.dt.uint8
+FP4 = mybir.dt.float4_e2m1fn_x4
+FP8 = mybir.dt.float8_e4m3fn_x4
+ALU = mybir.AluOpType
+ACT = mybir.ActivationFunctionType
+AX = mybir.AxisListType
+
+P = 128
+B, S, K, F, D = 256, 8, 1024, 1024, 2048
+NM = B * S
+G = 2
+FT = 8
+NU = 2 * FT
+HS = 64
+BANK = 512
+
+FLOPS = 2 * 2 * NM * K * F + 2 * B * F * D
+
+ON_G = (0, 2, 3, 4, 6, 8, 9, 10, 12, 13)
+STEP = (
+    ("sum_e", 2),
+    ("feature", 3),
+    ("add_prior", 0),
+    ("weight_v", 3),
+    ("sum_g", 4),
+    ("shift", 15),
+    ("maximum", 0),
+    ("take", 2),
+    ("turn", 5),
+    ("inv_u", 3),
+    ("square", 16),
+    ("relu", 3),
+    ("leave", 5),
+    ("mx_a", -1),
+    ("mx_v", 2),
+    ("project", 14),
+    ("quant", 5),
+    ("exponent", 1),
+    ("div_u", 4),
+    ("weight_g", 3),
+    ("subtract", 0),
+)
+FIN0 = 22
+BANKS = (3, 2, 1)
+
+
+def tile_attentive_set_pool_f2_kernel(
+    tc, x_words, x_scales, wv_words, wv_scales, wa_words, wa_scales, b, prior, wo_words, wo_scales, c, gain, out
+):
+    nc = tc.nc
+    with ExitStack() as ctx:
+        keep = ctx.enter_context(tc.tile_pool(name="keep", bufs=1))
+        work = ctx.enter_context(tc.tile_pool(name="work", bufs=3))
+        ps = ctx.enter_context(tc.psum_pool(name="ps", bufs=1))
+        ctx.enter_context(tc.manual_schedule())
+
+        def const(shape, dtype, name):
+            t = keep.tile(shape, dtype, name=name, tag=name, bufs=1, align_bytes=64)
+            return t
+
+        xw = [const([P, G, NM], U8, "xw0"), const([P, G, NM], U8, "xw1")]
+        wa_first, wa_rest = const([P, G, 512], U8, "wa0"), const([P, G, 1536], U8, "wa1")
+        wv = const([P, G, 2 * F], U8, "wv")
+        wo = const([P, G, 2 * D], U8, "wo")
+        xs, was = const([P, G * NM], U8, "xs"), const([P, G * F], U8, "was")
+        wvs, wos = const([P, G * F], U8, "wvs"), const([P, G * D], U8, "wos")
+        prow, brow, ones = const([P, NM], BF16, "prow"), const([P, P], BF16, "brow"), const([P, P], BF16, "ones")
+        ident, identb = const([P, P], F32, "ident"), const([P, P], BF16, "identb")
+        pr = const([P, 4, 4, HS, 2], F32, "pr")
+        bcol = const([P, FT], F32, "bcol")
+        cb, gb = const([P, D], BF16, "cb"), const([P, D], BF16, "gb")
+        dummy, neghalf = const([P, 1], F32, "dummy"), const([P, 1], F32, "neghalf")
+
+        nc.vector.memset(dummy[:], 0.0)
+        nc.vector.memset(prow[:].bitcast(U32), 0)
+        nc.vector.memset(was[:].bitcast(I32), 0)
+        nc.vector.memset(xs[:].bitcast(I32), 0)
+        nc.vector.memset(ones[:], 1.0)
+        nc.vector.memset(brow[:].bitcast(U32), 0)
+        nc.vector.memset(wvs[:].bitcast(I32), 0)
+        nc.vector.memset(wos[:].bitcast(I32), 0)
+        nc.vector.memset(neghalf[:], -0.5)
+        nc.scalar.activation(out=dummy[:], in_=dummy[:], func=ACT.Exp)
+
+        def words(tile, dram, lo, hi):
+            nc.sync.dma_start(out=tile[:], in_=dram.rearrange("g p c -> p g c")[:, :, lo:hi])
+
+        def scales(eng, tile, dram, q):
+            eng.dma_start(
+                out=tile[32 * q : 32 * q + 4, :].bitcast(I32).rearrange("p (g n) -> p g n", g=G),
+                in_=dram[:, 4 * q : 4 * q + 4, :].bitcast(I32).rearrange("g q n -> q g n"),
+            )
+
+        words(wa_first, wa_words, 0, 512)
+        words(xw[0], x_words, 0, 2048)
+        nc.gpsimd.dma_start(out=prow[0:1, :], in_=prior.rearrange("(o s) j -> o (s j)", o=1))
+        for q in range(4):
+            scales(nc.scalar, xs, x_scales, q)
+        for q in range(2):
+            scales(nc.scalar, was, wa_scales, q)
+        for q in range(2, 4):
+            scales(nc.gpsimd, was, wa_scales, q)
+        words(wa_rest, wa_words, 512, 2048)
+        nc.scalar.dma_start(out=brow[0:FT, :], in_=b.rearrange("(c p) -> c p", c=FT))
+        make_identity(nc, identb[:])
+        make_identity(nc, ident[:])
+        for q in range(4):
+            scales(nc.sync, wvs, wv_scales, q)
+        words(wv, wv_words, 0, 2048)
+        words(xw[1], x_words, 2048, 4096)
+        for q in range(4):
+            scales(nc.sync, wos, wo_scales, q)
+        words(wo, wo_words, 0, 4096)
+        nc.sync.dma_start(out=cb[:], in_=c.partition_broadcast(P))
+        nc.sync.dma_start(out=gb[:], in_=gain.partition_broadcast(P))
+
+        def bank(tag, bufs):
+            t = ps.tile([P, BANK], F32, name=tag, tag=tag, bufs=bufs)
+            return t
+
+        for h in range(4):
+            pp = bank("av"[h % 2], BANKS[h % 2])
+            nc.tensor.matmul(pp[:], lhsT=ones[:], rhs=prow[:, BANK * h : BANK * h + BANK], start=True, stop=True)
+            src = pp[:].rearrange("p (i a l) -> p a i l", a=4, l=2)
+            if h % 2 == 0:
+                nc.vector.tensor_copy(out=pr[:, h], in_=src)
+            else:
+                nc.scalar.copy(out=pr[:, h], in_=src)
+
+        at, vt, lt, mt, et, gt, ht = {}, {}, {}, {}, {}, {}, {}
+        Et, Nt, rt, pot = {}, {}, {}, {}
+        btt, ptt, codes, cscale = {}, {}, {}, {}
+
+        def mx(u, w, lo, s, h, tag):
+            st, ft = divmod(u, FT)
+            acc = bank(tag, BANKS[0] if tag == "a" else BANKS[1])
+            n0 = BANK * h
+            for g in range(G):
+                nc.tensor.matmul_mx(
+                    out=acc[:],
+                    lhsT=w[:, g, 256 * (ft - lo) : 256 * (ft - lo) + 256].bitcast(FP4),
+                    lhsT_scale=s[:, F * g + P * ft : F * g + P * ft + P],
+                    rhs=xw[st][:, g, 2 * n0 : 2 * n0 + 1024].bitcast(FP4),
+                    rhs_scale=xs[:, NM * g + 1024 * st + n0 : NM * g + 1024 * st + n0 + BANK],
+                    start=(g == 0),
+                    stop=(g == G - 1),
+                )
+            return acc
+
+        def mx_a(u):
+            for h in range(2):
+                if u % FT < 2:
+                    at[u, h] = mx(u, wa_first, 0, was, h, "a")
+                else:
+                    at[u, h] = mx(u, wa_rest, 2, was, h, "a")
+
+        def mx_v(u):
+            for h in range(2):
+                vt[u, h] = mx(u, wv, 0, wvs, h, "v")
+
+        def add_prior(u):
+            for h in range(2):
+                l = work.tile([P, 4, HS, 2], F32, name="l", tag="l", bufs=8, align_bytes=64)
+                lt[u, h] = l
+                nc.vector.tensor_tensor(
+                    out=l[:],
+                    in0=at[u, h][:].rearrange("p (i a l) -> p a i l", a=4, l=2),
+                    in1=pr[:, 2 * (u // FT) + h],
+                    op=ALU.add,
+                )
+
+        def maximum(u):
+            for h in range(2):
+                m = work.tile([P, HS], F32, name="m", tag="m", bufs=6, align_bytes=64)
+                mt[u, h] = m
+                nc.vector.tensor_reduce(
+                    out=m[:], in_=lt[u, h][:].rearrange("p a i l -> p i a l"), axis=AX.XY, op=ALU.max
+                )
+
+        def subtract(u):
+            for h in range(2):
+                l = lt[u, h]
+                nc.gpsimd.tensor_tensor(
+                    out=l[:],
+                    in0=l[:],
+                    in1=mt[u, h][:].unsqueeze(1).unsqueeze(3).to_broadcast([P, 4, HS, 2]),
+                    op=ALU.subtract,
+                )
+
+        def exponent(u):
+            e = work.tile([P, S, P], F32, name="e", tag="e", bufs=5, align_bytes=64)
+            et[u] = e
+            for h in range(2):
+                nc.scalar.activation(
+                    out=e[:, :, HS * h : HS * h + HS].rearrange("p (a l) i -> p a l i", l=2),
+                    in_=lt[u, h][:].rearrange("p a i l -> p a l i"),
+                    func=ACT.Exp,
+                )
+
+        def new_g(u):
+            g = work.tile([P, S, P], F32, name="g", tag="g", bufs=4, align_bytes=64)
+            gt[u] = g
+            return g
+
+        def weight_v(u):
+            if u in ON_G:
+                return
+            g = new_g(u)
+            for h in range(2):
+                r = slice(HS * h, HS * h + HS)
+                nc.vector.scalar_tensor_tensor(
+                    out=g[:, :, r],
+                    in0=vt[u, h][:].rearrange("p (i j) -> p j i", j=S),
+                    scalar=bcol[:, u % FT : u % FT + 1],
+                    in1=et[u][:, :, r],
+                    op0=ALU.add,
+                    op1=ALU.mult,
+                )
+
+        def relu(u):
+            if u in ON_G:
+                return
+            g = gt[u]
+            if u == NU - 1:
+                for h in range(2):
+                    r = slice(HS * h, HS * h + HS)
+                    nc.scalar.activation(out=g[:, :, r], in_=g[:, :, r], func=ACT.Relu)
+            else:
+                nc.scalar.activation(out=g[:], in_=g[:], func=ACT.Relu)
+
+        def feature(u):
+            if u not in ON_G:
+                return
+            f = work.tile([P, S, P], F32, name="f", tag="f", bufs=2, align_bytes=64)
+            ht[u] = f
+            for h in range(2):
+                nc.scalar.activation(
+                    out=f[:, :, HS * h : HS * h + HS],
+                    in_=vt[u, h][:].rearrange("p (i j) -> p j i", j=S),
+                    func=ACT.Relu,
+                    bias=bcol[:, u % FT : u % FT + 1],
+                )
+
+        def weight_g(u):
+            if u not in ON_G:
+                return
+            g = new_g(u)
+            nc.gpsimd.tensor_tensor(out=g[:], in0=ht[u][:], in1=et[u][:], op=ALU.mult)
+
+        def sums(u, src, store, tag, bufs):
+            f = u % 4
+            if f == 0:
+                store[u // 4] = bank(tag, bufs)
+            for j in range(S):
+                nc.tensor.matmul(
+                    store[u // 4][:, P * f : P * f + P],
+                    lhsT=src[u][:, j, :],
+                    rhs=ident[:],
+                    is_transpose=True,
+                    start=(j == 0),
+                    stop=(j == S - 1),
+                )
+
+        def sum_e(u):
+            sums(u, et, Et, "E", 1)
+
+        def sum_g(u):
+            sums(u, gt, Nt, "N", BANKS[2])
+
+        def new_po(q):
+            po = work.tile([P, 4, P], BF16, name="po", tag="po", bufs=2, align_bytes=64)
+            pot[q] = po
+
+        def take(u):
+            f = u % 4
+            r = work.tile([P, 4, 32], F32, name="r", tag="r", bufs=4, align_bytes=64)
+            rt["u", u] = r
+            nc.scalar.copy(out=r[:], in_=Et[u // 4][:, P * f : P * f + P].rearrange("s (p t) -> s t p", t=4))
+
+        def inv_u(u):
+            r = rt["u", u]
+            nc.vector.reciprocal(out=r[:], in_=r[:])
+
+        def div_u(u):
+            f, q = u % 4, u // 4
+            if f == 0:
+                new_po(q)
+            nc.vector.tensor_tensor(
+                out=pot[q][:, :, 32 * f : 32 * f + 32],
+                in0=Nt[q][:, P * f : P * f + P].rearrange("s (p t) -> s t p", t=4),
+                in1=rt["u", u][:],
+                op=ALU.mult,
+            )
+
+        def turn(q):
+            bt = ps.tile([P, 4, P], BF16, name="bt", tag="misc", bufs=1)
+            btt[q] = bt
+            for t in range(4):
+                nc.tensor.transpose(bt[:, t, :], pot[q][:, t, :], identb[:])
+
+        def leave(q, eng):
+            pt = work.tile([P, P, 4], BF16, name="pt", tag="pt", bufs=2, align_bytes=64)
+            ptt[q] = pt
+            if eng == "S":
+                nc.scalar.copy(out=pt[:], in_=btt[q][:].rearrange("p t n -> p n t"))
+            else:
+                nc.vector.tensor_copy(out=pt[:], in_=btt[q][:].rearrange("p t n -> p n t"))
+
+        def quant(q):
+            cd = work.tile([P, P], U32, name="cd", tag="cd", bufs=4, align_bytes=64)
+            cs = work.tile([P, P], U8, name="cs", tag="cs", bufs=4, align_bytes=64)
+            nc.vector.quantize_mx(out=cd[:].bitcast(FP8), scales=cs[:], in_=ptt[q][:].rearrange("p n t -> p (n t)"))
+            codes[q], cscale[q] = cd, cs
+
+        yt, sst, zt, rst = {}, {}, {}, {}
+
+        def project(st, nt, tag, bufs):
+            acc = bank(tag, bufs)
+            for g in range(G):
+                q = 2 * st + g
+                nc.tensor.matmul_mx(
+                    out=acc[:],
+                    lhsT=codes[q][:].bitcast(FP8),
+                    lhsT_scale=cscale[q][:],
+                    rhs=wo[:, g, 1024 * nt : 1024 * nt + 1024].bitcast(FP4),
+                    rhs_scale=wos[:, D * g + BANK * nt : D * g + BANK * nt + BANK],
+                    start=(g == 0),
+                    stop=(g == G - 1),
+                )
+            zt[st, nt] = acc
+
+        def shift(st, nt):
+            if nt == 0:
+                ss = work.tile([P, 4], F32, name="ss", tag="ss", bufs=2, align_bytes=64)
+                sst[st] = ss
+            y = work.tile([P, BANK], F32, name="y", tag="y", bufs=8, align_bytes=64)
+            yt[st, nt] = y
+            nc.vector.tensor_tensor(out=y[:], in0=zt[st, nt][:], in1=cb[:, BANK * nt : BANK * nt + BANK], op=ALU.add)
+
+        def square(st, nt):
+            sq = work.tile([P, BANK], BF16, name="sq", tag="sq", bufs=2, align_bytes=64)
+            nc.scalar.activation(out=sq[:], in_=yt[st, nt][:], func=ACT.Square, accum_out=sst[st][:, nt : nt + 1])
+
+        def norm(st):
+            ms = work.tile([P, 1], F32, name="ms", tag="ms", bufs=2, align_bytes=64)
+            rs = work.tile([P, 1], F32, name="rs", tag="rs", bufs=2, align_bytes=64)
+            rst[st] = rs
+            nc.vector.tensor_reduce(out=ms[:], in_=sst[st][:], axis=AX.X, op=ALU.add)
+            nc.vector.tensor_scalar(out=ms[:], in0=ms[:], scalar1=1.0 / D, scalar2=None, op0=ALU.mult)
+            nc.gpsimd.tensor_tensor(out=rs[:], in0=ms[:], in1=neghalf[:], op=ALU.pow)
+
+        def gain_v(st, nt):
+            y = yt[st, nt]
+            nc.vector.tensor_tensor(out=y[:], in0=y[:], in1=gb[:, BANK * nt : BANK * nt + BANK], op=ALU.mult)
+
+        def gain_g(st, nt):
+            y = yt[st, nt]
+            nc.gpsimd.tensor_tensor(out=y[:], in0=y[:], in1=gb[:, BANK * nt : BANK * nt + BANK], op=ALU.mult)
+
+        def store(st, nt):
+            nc.sync.dma_start(out=out[P * st : P * st + P, BANK * nt : BANK * nt + BANK], in_=yt[st, nt][:])
+
+        def scale_out(st, nt, eng):
+            y = yt[st, nt]
+            if eng == "S":
+                nc.scalar.activation(out=y[:], in_=y[:], func=ACT.Copy, scale=rst[st][:])
+            else:
+                nc.vector.tensor_scalar(out=y[:], in0=y[:], scalar1=rst[st][:], scalar2=None, op0=ALU.mult)
+            store(st, nt)
+
+        def finish(st, nt):
+            y = yt[st, nt]
+            nc.vector.scalar_tensor_tensor(
+                out=y[:], in0=y[:], scalar=rst[st][:], in1=gb[:, BANK * nt : BANK * nt + BANK], op0=ALU.mult, op1=ALU.mult
+            )
+            store(st, nt)
+
+        def subtract_last(u):
+            for h in range(2):
+                l = lt[u, h]
+                m = mt[u, h][:].unsqueeze(1).unsqueeze(3).to_broadcast([P, 4, HS, 2])
+                if h == 0:
+                    nc.gpsimd.tensor_tensor(out=l[:], in0=l[:], in1=m, op=ALU.subtract)
+                else:
+                    nc.vector.tensor_tensor(out=l[:], in0=l[:], in1=m, op=ALU.subtract)
+
+        stage = {
+            "sum_e": sum_e,
+            "take": take,
+            "inv_u": inv_u,
+            "div_u": div_u,
+            "sum_g": sum_g,
+            "mx_a": mx_a,
+            "mx_v": mx_v,
+            "add_prior": add_prior,
+            "weight_v": weight_v,
+            "maximum": maximum,
+            "weight_g": weight_g,
+            "subtract": subtract,
+            "feature": feature,
+            "exponent": exponent,
+            "relu": relu,
+        }
+        half_stage = {
+            "turn": turn,
+            "leave": lambda q: leave(q, "S"),
+            "quant": quant,
+        }
+        proj_stage = {
+            "project": lambda nt: project(0, nt, "misc", 1),
+            "shift": lambda nt: shift(0, nt),
+            "square": lambda nt: square(0, nt),
+        }
+
+        mx_a(0)
+        bp = bank("misc", 1)
+        nc.tensor.matmul(bp[:, 0:FT], lhsT=brow[:], rhs=identb[:, 0:FT], start=True, stop=True)
+        nc.vector.tensor_copy(out=bcol[:], in_=bp[:, 0:FT])
+        last = max(NU - 1 + max(back for name, back in STEP if name in stage), FIN0 + 2)
+        for k in range(last + 1):
+            for name, back in STEP:
+                if name in stage:
+                    u = k - back
+                    if 0 <= u < NU and not (name == "mx_a" and u == 0) and not (name == "div_u" and u == NU - 1):
+                        if name == "subtract" and u == NU - 1:
+                            subtract_last(u)
+                        else:
+                            stage[name](u)
+                elif name in half_stage:
+                    q, rem = divmod(k - back - 3, 4)
+                    if rem == 0 and 0 <= q < 3:
+                        half_stage[name](q)
+                else:
+                    if 0 <= k - back < 4:
+                        proj_stage[name](k - back)
+            if k == FIN0:
+                norm(0)
+            if 0 <= k - FIN0 - 1 < 2 :
+                finish(0, 2 * (k - FIN0 - 1))
+                finish(0, 2 * (k - FIN0 - 1) + 1)
+        div_u(NU - 1)
+        turn(3)
+        leave(3, "V")
+        quant(3)
+        for nt in range(4):
+            project(1, nt, "av"[nt % 2], BANKS[nt % 2])
+        for nt in range(4):
+            shift(1, nt)
+            square(1, nt)
+        gain_g(1, 0)
+        gain_g(1, 1)
+        gain_v(1, 2)
+        norm(1)
+        gain_v(1, 3)
+        for nt in range(4):
+            scale_out(1, nt, "VS"[nt % 2])

@@ -25,32 +25,33 @@ BANK = 512
 
 FLOPS = 2 * 2 * NM * K * F + 2 * B * F * D
 
-ON_G = (0, 2, 3, 4, 6, 8, 9, 10, 12, 13)
+ON_G = (1, 2, 6, 9, 10, 12, 13)
 STEP = (
-    ("sum_e", 2),
-    ("feature", 3),
-    ("add_prior", 0),
     ("weight_v", 3),
+    ("feature", 3),
     ("sum_g", 4),
+    ("sum_e", 2),
     ("shift", 15),
-    ("maximum", 0),
-    ("take", 2),
+    ("square", 15),
     ("turn", 5),
-    ("inv_u", 3),
-    ("square", 16),
-    ("relu", 3),
-    ("leave", 5),
-    ("mx_a", -1),
     ("mx_v", 2),
+    ("relu", 3),
+    ("add_prior", 0),
+    ("maximum", 0),
+    ("leave", 5),
     ("project", 14),
-    ("quant", 5),
-    ("exponent", 1),
+    ("inv_u", 3),
     ("div_u", 4),
+    ("quant", 5),
     ("weight_g", 3),
+    ("exponent", 1),
     ("subtract", 0),
+    ("mx_a", -1),
+    ("take", 2),
 )
-FIN0 = 22
-BANKS = (3, 2, 1)
+FIN0 = 21
+BANKS = (2, 2, 2)
+LN = (1,)
 
 
 def tile_attentive_set_pool_f2_kernel(
@@ -136,7 +137,7 @@ def tile_attentive_set_pool_f2_kernel(
             else:
                 nc.scalar.copy(out=pr[:, h], in_=src)
 
-        at, vt, lt, mt, et, gt, ht = {}, {}, {}, {}, {}, {}, {}
+        at, vt, lt, mt, dt, et, gt, ht = {}, {}, {}, {}, {}, {}, {}, {}
         Et, Nt, rt, pot = {}, {}, {}, {}
         btt, ptt, codes, cscale = {}, {}, {}, {}
 
@@ -188,11 +189,13 @@ def tile_attentive_set_pool_f2_kernel(
 
         def subtract(u):
             for h in range(2):
-                l = lt[u, h]
-                nc.gpsimd.tensor_tensor(
-                    out=l[:],
-                    in0=l[:],
-                    in1=mt[u, h][:].unsqueeze(1).unsqueeze(3).to_broadcast([P, 4, HS, 2]),
+                d = work.tile([P, S, HS], F32, name="d", tag="d", bufs=6, align_bytes=64)
+                dt[u, h] = d
+                eng = nc.vector if u == NU - 1 and h == 1 else nc.gpsimd
+                eng.tensor_tensor(
+                    out=d[:].rearrange("p (a l) i -> p a l i", l=2),
+                    in0=lt[u, h][:].rearrange("p a i l -> p a l i"),
+                    in1=mt[u, h][:].unsqueeze(1).unsqueeze(1).to_broadcast([P, 4, 2, HS]),
                     op=ALU.subtract,
                 )
 
@@ -200,11 +203,7 @@ def tile_attentive_set_pool_f2_kernel(
             e = work.tile([P, S, P], F32, name="e", tag="e", bufs=5, align_bytes=64)
             et[u] = e
             for h in range(2):
-                nc.scalar.activation(
-                    out=e[:, :, HS * h : HS * h + HS].rearrange("p (a l) i -> p a l i", l=2),
-                    in_=lt[u, h][:].rearrange("p a i l -> p a l i"),
-                    func=ACT.Exp,
-                )
+                nc.scalar.activation(out=e[:, :, HS * h : HS * h + HS], in_=dt[u, h][:], func=ACT.Exp)
 
         def new_g(u):
             g = work.tile([P, S, P], F32, name="g", tag="g", bufs=4, align_bytes=64)
@@ -282,16 +281,33 @@ def tile_attentive_set_pool_f2_kernel(
 
         def take(u):
             f = u % 4
+            if u // 4 in LN:
+                if f == 3:
+                    q = u // 4
+                    r = work.tile([P, 4, P], F32, name="rq", tag="rq", bufs=2, align_bytes=64)
+                    rt[q] = r
+                    nc.scalar.activation(out=r[:], in_=Et[q][:].rearrange("s (p t) -> s t p", t=4), func=ACT.Ln)
+                    nc.scalar.activation(out=r[:], in_=r[:], func=ACT.Exp, scale=-1.0)
+                return
             r = work.tile([P, 4, 32], F32, name="r", tag="r", bufs=4, align_bytes=64)
             rt["u", u] = r
             nc.scalar.copy(out=r[:], in_=Et[u // 4][:, P * f : P * f + P].rearrange("s (p t) -> s t p", t=4))
 
         def inv_u(u):
+            if u // 4 in LN:
+                return
             r = rt["u", u]
             nc.vector.reciprocal(out=r[:], in_=r[:])
 
         def div_u(u):
             f, q = u % 4, u // 4
+            if q in LN:
+                if f == 3:
+                    new_po(q)
+                    nc.vector.tensor_tensor(
+                        out=pot[q][:], in0=Nt[q][:].rearrange("s (p t) -> s t p", t=4), in1=rt[q][:], op=ALU.mult
+                    )
+                return
             if f == 0:
                 new_po(q)
             nc.vector.tensor_tensor(
@@ -358,13 +374,11 @@ def tile_attentive_set_pool_f2_kernel(
             nc.vector.tensor_scalar(out=ms[:], in0=ms[:], scalar1=1.0 / D, scalar2=None, op0=ALU.mult)
             nc.gpsimd.tensor_tensor(out=rs[:], in0=ms[:], in1=neghalf[:], op=ALU.pow)
 
-        def gain_v(st, nt):
+        def gain(st, nt, eng):
             y = yt[st, nt]
-            nc.vector.tensor_tensor(out=y[:], in0=y[:], in1=gb[:, BANK * nt : BANK * nt + BANK], op=ALU.mult)
-
-        def gain_g(st, nt):
-            y = yt[st, nt]
-            nc.gpsimd.tensor_tensor(out=y[:], in0=y[:], in1=gb[:, BANK * nt : BANK * nt + BANK], op=ALU.mult)
+            yg = work.tile([P, BANK], F32, name="yg", tag="yg", bufs=4, align_bytes=64)
+            yt[st, nt] = yg
+            eng.tensor_tensor(out=yg[:], in0=y[:], in1=gb[:, BANK * nt : BANK * nt + BANK], op=ALU.mult)
 
         def store(st, nt):
             nc.sync.dma_start(out=out[P * st : P * st + P, BANK * nt : BANK * nt + BANK], in_=yt[st, nt][:])
@@ -383,15 +397,6 @@ def tile_attentive_set_pool_f2_kernel(
                 out=y[:], in0=y[:], scalar=rst[st][:], in1=gb[:, BANK * nt : BANK * nt + BANK], op0=ALU.mult, op1=ALU.mult
             )
             store(st, nt)
-
-        def subtract_last(u):
-            for h in range(2):
-                l = lt[u, h]
-                m = mt[u, h][:].unsqueeze(1).unsqueeze(3).to_broadcast([P, 4, HS, 2])
-                if h == 0:
-                    nc.gpsimd.tensor_tensor(out=l[:], in0=l[:], in1=m, op=ALU.subtract)
-                else:
-                    nc.vector.tensor_tensor(out=l[:], in0=l[:], in1=m, op=ALU.subtract)
 
         stage = {
             "sum_e": sum_e,
@@ -431,10 +436,7 @@ def tile_attentive_set_pool_f2_kernel(
                 if name in stage:
                     u = k - back
                     if 0 <= u < NU and not (name == "mx_a" and u == 0) and not (name == "div_u" and u == NU - 1):
-                        if name == "subtract" and u == NU - 1:
-                            subtract_last(u)
-                        else:
-                            stage[name](u)
+                        stage[name](u)
                 elif name in half_stage:
                     q, rem = divmod(k - back - 3, 4)
                     if rem == 0 and 0 <= q < 3:
@@ -456,10 +458,10 @@ def tile_attentive_set_pool_f2_kernel(
         for nt in range(4):
             shift(1, nt)
             square(1, nt)
-        gain_g(1, 0)
-        gain_g(1, 1)
-        gain_v(1, 2)
+            if nt < 2:
+                gain(1, nt, nc.gpsimd)
+        gain(1, 2, nc.vector)
         norm(1)
-        gain_v(1, 3)
-        for nt in range(4):
-            scale_out(1, nt, "VS"[nt % 2])
+        gain(1, 3, nc.vector)
+        for nt in (2, 3, 0, 1):
+            scale_out(1, nt, "SV"[nt % 2])

@@ -25,33 +25,48 @@ BANK = 512
 
 FLOPS = 2 * 2 * NM * K * F + 2 * B * F * D
 
-ON_G = (1, 2, 6, 9, 10, 12, 13)
+SPLIT = (0, 1, 15)
+
+ON_G = (10, 13)
+ON_S = (2, 6, 14, 15)
 STEP = (
-    ("weight_v", 3),
-    ("feature", 3),
-    ("sum_g", 4),
-    ("sum_e", 2),
-    ("shift", 15),
-    ("square", 15),
-    ("turn", 5),
-    ("mx_v", 2),
-    ("relu", 3),
-    ("add_prior", 0),
-    ("maximum", 0),
-    ("leave", 5),
-    ("project", 14),
-    ("inv_u", 3),
-    ("div_u", 4),
-    ("quant", 5),
-    ("weight_g", 3),
-    ("exponent", 1),
-    ("subtract", 0),
-    ("mx_a", -1),
-    ("take", 2),
+    ("square", 22, (0, 1)),
+    ("mx_v", 2, (0, 1)),
+    ("add_prior", 0, (0,)),
+    ("mx_a", -1, (0,)),
+    ("feature", 3, (1,)),
+    ("relu", 4, (0, 1)),
+    ("weight_v", 3, (1,)),
+    ("add_prior", 0, (1,)),
+    ("shift", 15, (0, 1)),
+    ("sum_e", 2, (0, 1)),
+    ("inv_u", 3, (0, 1)),
+    ("turn", 5, (0, 1)),
+    ("weight_g", 3, (0, 1)),
+    ("feature", 2, (0,)),
+    ("weight_v", 2, (0,)),
+    ("weight_s", 3, (1,)),
+    ("leave", 5, (0, 1)),
+    ("sum_g", 4, (0, 1)),
+    ("quant", 7, (0, 1)),
+    ("maximum", 0, (0,)),
+    ("subtract", 0, (0,)),
+    ("mx_a", -1, (1,)),
+    ("weight_s", 2, (0,)),
+    ("maximum", 0, (1,)),
+    ("project", 14, (0, 1)),
+    ("div_u", 4, (0, 1)),
+    ("subtract", 0, (1,)),
+    ("exponent", 1, (0, 1)),
+    ("take", 2, (0, 1)),
 )
-FIN0 = 21
-BANKS = (2, 2, 2)
-LN = (1,)
+FIN0 = 34
+BANKS = (2, 3, 1)
+LN = (0, 1, 2)
+EP = (30, 29)
+
+
+HALVED = ("mx_a", "mx_v", "add_prior", "maximum", "subtract", "exponent", "weight_v", "weight_s", "feature")
 
 
 def tile_attentive_set_pool_f2_kernel(
@@ -68,29 +83,30 @@ def tile_attentive_set_pool_f2_kernel(
             t = keep.tile(shape, dtype, name=name, tag=name, bufs=1, align_bytes=64)
             return t
 
-        xw = [const([P, G, NM], U8, "xw0"), const([P, G, NM], U8, "xw1")]
+        xa, xb, xc = const([P, G, 1024], U8, "xa"), const([P, G, 1024], U8, "xb"), const([P, G, NM], U8, "xc")
         wa_first, wa_rest = const([P, G, 512], U8, "wa0"), const([P, G, 1536], U8, "wa1")
         wv = const([P, G, 2 * F], U8, "wv")
         wo = const([P, G, 2 * D], U8, "wo")
         xs, was = const([P, G * NM], U8, "xs"), const([P, G * F], U8, "was")
         wvs, wos = const([P, G * F], U8, "wvs"), const([P, G * D], U8, "wos")
-        prow, brow, ones = const([P, NM], BF16, "prow"), const([P, P], BF16, "brow"), const([P, P], BF16, "ones")
+        prow = [const([P, 2 * BANK], BF16, "prow0"), const([P, 2 * BANK], BF16, "prow1")]
+        brow, ones = const([P, P], BF16, "brow"), const([P, P], BF16, "ones")
         ident, identb = const([P, P], F32, "ident"), const([P, P], BF16, "identb")
         pr = const([P, 4, 4, HS, 2], F32, "pr")
         bcol = const([P, FT], F32, "bcol")
         cb, gb = const([P, D], BF16, "cb"), const([P, D], BF16, "gb")
         dummy, neghalf = const([P, 1], F32, "dummy"), const([P, 1], F32, "neghalf")
 
-        nc.vector.memset(dummy[:], 0.0)
-        nc.vector.memset(prow[:].bitcast(U32), 0)
         nc.vector.memset(was[:].bitcast(I32), 0)
         nc.vector.memset(xs[:].bitcast(I32), 0)
+        nc.vector.memset(prow[0][:].bitcast(U32), 0)
+        nc.vector.memset(dummy[:], 0.0)
         nc.vector.memset(ones[:], 1.0)
         nc.vector.memset(brow[:].bitcast(U32), 0)
+        nc.vector.memset(prow[1][:].bitcast(U32), 0)
         nc.vector.memset(wvs[:].bitcast(I32), 0)
         nc.vector.memset(wos[:].bitcast(I32), 0)
         nc.vector.memset(neghalf[:], -0.5)
-        nc.scalar.activation(out=dummy[:], in_=dummy[:], func=ACT.Exp)
 
         def words(tile, dram, lo, hi):
             nc.sync.dma_start(out=tile[:], in_=dram.rearrange("g p c -> p g c")[:, :, lo:hi])
@@ -101,23 +117,25 @@ def tile_attentive_set_pool_f2_kernel(
                 in_=dram[:, 4 * q : 4 * q + 4, :].bitcast(I32).rearrange("g q n -> q g n"),
             )
 
-        words(wa_first, wa_words, 0, 512)
-        words(xw[0], x_words, 0, 2048)
-        nc.gpsimd.dma_start(out=prow[0:1, :], in_=prior.rearrange("(o s) j -> o (s j)", o=1))
+        prior_row = prior.rearrange("(o s) j -> o (s j)", o=1)
         for q in range(4):
-            scales(nc.scalar, xs, x_scales, q)
-        for q in range(2):
             scales(nc.scalar, was, wa_scales, q)
-        for q in range(2, 4):
-            scales(nc.gpsimd, was, wa_scales, q)
-        words(wa_rest, wa_words, 512, 2048)
-        nc.scalar.dma_start(out=brow[0:FT, :], in_=b.rearrange("(c p) -> c p", c=FT))
+        for q in range(4):
+            scales(nc.sync, xs, x_scales, q)
+        words(wa_first, wa_words, 0, 512)
+        words(xa, x_words, 0, 1024)
+        words(xb, x_words, 1024, 2048)
+        nc.scalar.dma_start(out=prow[0][0:1, :], in_=prior_row[:, 0 : 2 * BANK])
+        nc.scalar.activation(out=dummy[:], in_=dummy[:], func=ACT.Exp)
         make_identity(nc, identb[:])
         make_identity(nc, ident[:])
+        nc.gpsimd.dma_start(out=brow[0:FT, :], in_=b.rearrange("(c p) -> c p", c=FT))
+        nc.gpsimd.dma_start(out=prow[1][0:1, :], in_=prior_row[:, 2 * BANK : 4 * BANK])
+        words(wa_rest, wa_words, 512, 2048)
         for q in range(4):
             scales(nc.sync, wvs, wv_scales, q)
         words(wv, wv_words, 0, 2048)
-        words(xw[1], x_words, 2048, 4096)
+        words(xc, x_words, 2048, 4096)
         for q in range(4):
             scales(nc.sync, wos, wo_scales, q)
         words(wo, wo_words, 0, 4096)
@@ -128,18 +146,32 @@ def tile_attentive_set_pool_f2_kernel(
             t = ps.tile([P, BANK], F32, name=tag, tag=tag, bufs=bufs)
             return t
 
-        for h in range(4):
-            pp = bank("av"[h % 2], BANKS[h % 2])
-            nc.tensor.matmul(pp[:], lhsT=ones[:], rhs=prow[:, BANK * h : BANK * h + BANK], start=True, stop=True)
+        def spread_prior(h, tag, bufs, eng):
+            pp = bank(tag, bufs)
+            n0 = BANK * (h % 2)
+            nc.tensor.matmul(pp[:], lhsT=ones[:], rhs=prow[h // 2][:, n0 : n0 + BANK], start=True, stop=True)
             src = pp[:].rearrange("p (i a l) -> p a i l", a=4, l=2)
-            if h % 2 == 0:
+            if eng == "V":
                 nc.vector.tensor_copy(out=pr[:, h], in_=src)
             else:
                 nc.scalar.copy(out=pr[:, h], in_=src)
 
+        spread_prior(0, "v", BANKS[1], "V")
+        spread_prior(1, "v", BANKS[1], "S")
+
+        def spread_bias():
+            bp = bank("misc", 1)
+            nc.tensor.matmul(bp[:, 0:FT], lhsT=brow[:], rhs=identb[:, 0:FT], start=True, stop=True)
+            nc.scalar.copy(out=bcol[:], in_=bp[:, 0:FT])
+
         at, vt, lt, mt, dt, et, gt, ht = {}, {}, {}, {}, {}, {}, {}, {}
         Et, Nt, rt, pot = {}, {}, {}, {}
         btt, ptt, codes, cscale = {}, {}, {}, {}
+
+        def members(st, h):
+            if st == 0:
+                return (xa, xb)[h][:]
+            return xc[:, :, 1024 * h : 1024 * h + 1024]
 
         def mx(u, w, lo, s, h, tag):
             st, ft = divmod(u, FT)
@@ -150,71 +182,82 @@ def tile_attentive_set_pool_f2_kernel(
                     out=acc[:],
                     lhsT=w[:, g, 256 * (ft - lo) : 256 * (ft - lo) + 256].bitcast(FP4),
                     lhsT_scale=s[:, F * g + P * ft : F * g + P * ft + P],
-                    rhs=xw[st][:, g, 2 * n0 : 2 * n0 + 1024].bitcast(FP4),
+                    rhs=members(st, h)[:, g, :].bitcast(FP4),
                     rhs_scale=xs[:, NM * g + 1024 * st + n0 : NM * g + 1024 * st + n0 + BANK],
                     start=(g == 0),
                     stop=(g == G - 1),
                 )
             return acc
 
-        def mx_a(u):
-            for h in range(2):
+        def mx_a(u, hs):
+            for h in hs:
                 if u % FT < 2:
                     at[u, h] = mx(u, wa_first, 0, was, h, "a")
                 else:
                     at[u, h] = mx(u, wa_rest, 2, was, h, "a")
 
-        def mx_v(u):
-            for h in range(2):
+        def mx_v(u, hs):
+            for h in hs:
                 vt[u, h] = mx(u, wv, 0, wvs, h, "v")
 
-        def add_prior(u):
-            for h in range(2):
-                l = work.tile([P, 4, HS, 2], F32, name="l", tag="l", bufs=8, align_bytes=64)
-                lt[u, h] = l
+        def runs(u, hs):
+            if hs == (0, 1) and u not in SPLIT:
+                return [(0, P)]
+            return [(HS * h, HS * h + HS) for h in hs]
+
+        def new(store, u, hs, shape, name, bufs):
+            if 0 in hs:
+                t = work.tile(shape, F32, name=name, tag=name, bufs=bufs, align_bytes=64)
+                store[u] = t
+            return store[u]
+
+        def add_prior(u, hs):
+            l = new(lt, u, hs, [P, 4, P, 2], "l", 4)
+            for h in hs:
                 nc.vector.tensor_tensor(
-                    out=l[:],
+                    out=l[:, :, HS * h : HS * h + HS, :],
                     in0=at[u, h][:].rearrange("p (i a l) -> p a i l", a=4, l=2),
                     in1=pr[:, 2 * (u // FT) + h],
                     op=ALU.add,
                 )
 
-        def maximum(u):
-            for h in range(2):
-                m = work.tile([P, HS], F32, name="m", tag="m", bufs=6, align_bytes=64)
-                mt[u, h] = m
+        def maximum(u, hs):
+            m = new(mt, u, hs, [P, P], "m", 3)
+            for lo, hi in runs(u, hs):
                 nc.vector.tensor_reduce(
-                    out=m[:], in_=lt[u, h][:].rearrange("p a i l -> p i a l"), axis=AX.XY, op=ALU.max
+                    out=m[:, lo:hi], in_=lt[u][:, :, lo:hi, :].rearrange("p a i l -> p i a l"), axis=AX.XY, op=ALU.max
                 )
 
-        def subtract(u):
-            for h in range(2):
-                d = work.tile([P, S, HS], F32, name="d", tag="d", bufs=6, align_bytes=64)
-                dt[u, h] = d
-                eng = nc.vector if u == NU - 1 and h == 1 else nc.gpsimd
+        def subtract(u, hs):
+            d = new(dt, u, hs, [P, S, P], "d", 3)
+            for lo, hi in runs(u, hs):
+                eng = nc.vector if u == NU - 1 and lo > 0 else nc.gpsimd
                 eng.tensor_tensor(
-                    out=d[:].rearrange("p (a l) i -> p a l i", l=2),
-                    in0=lt[u, h][:].rearrange("p a i l -> p a l i"),
-                    in1=mt[u, h][:].unsqueeze(1).unsqueeze(1).to_broadcast([P, 4, 2, HS]),
+                    out=d[:, :, lo:hi].rearrange("p (a l) i -> p a l i", l=2),
+                    in0=lt[u][:, :, lo:hi, :].rearrange("p a i l -> p a l i"),
+                    in1=mt[u][:, lo:hi].unsqueeze(1).unsqueeze(1).to_broadcast([P, 4, 2, hi - lo]),
                     op=ALU.subtract,
                 )
 
-        def exponent(u):
-            e = work.tile([P, S, P], F32, name="e", tag="e", bufs=5, align_bytes=64)
-            et[u] = e
-            for h in range(2):
-                nc.scalar.activation(out=e[:, :, HS * h : HS * h + HS], in_=dt[u, h][:], func=ACT.Exp)
+        def exponent(u, hs):
+            e = new(et, u, hs, [P, S, P], "e", 5)
+            for lo, hi in runs(u, hs):
+                nc.scalar.activation(out=e[:, :, lo:hi], in_=dt[u][:, :, lo:hi], func=ACT.Exp)
+            if u == NU - 1 and 1 in hs:
+                nc.scalar.activation(out=dummy[:], in_=dummy[:], func=ACT.Abs_reciprocal_sqrt)
 
         def new_g(u):
             g = work.tile([P, S, P], F32, name="g", tag="g", bufs=4, align_bytes=64)
             gt[u] = g
             return g
 
-        def weight_v(u):
-            if u in ON_G:
+        def weight_v(u, hs):
+            if u in ON_G or u in ON_S:
                 return
-            g = new_g(u)
-            for h in range(2):
+            if 0 in hs:
+                new_g(u)
+            g = gt[u]
+            for h in hs:
                 r = slice(HS * h, HS * h + HS)
                 nc.vector.scalar_tensor_tensor(
                     out=g[:, :, r],
@@ -225,8 +268,18 @@ def tile_attentive_set_pool_f2_kernel(
                     op1=ALU.mult,
                 )
 
+        def weight_s(u, hs):
+            if u not in ON_S:
+                return
+            if 0 in hs:
+                new_g(u)
+            for lo, hi in runs(u, hs):
+                nc.vector.tensor_tensor(
+                    out=gt[u][:, :, lo:hi], in0=ht[u][:, :, lo:hi], in1=et[u][:, :, lo:hi], op=ALU.mult
+                )
+
         def relu(u):
-            if u in ON_G:
+            if u in ON_G or u in ON_S:
                 return
             g = gt[u]
             if u == NU - 1:
@@ -236,12 +289,14 @@ def tile_attentive_set_pool_f2_kernel(
             else:
                 nc.scalar.activation(out=g[:], in_=g[:], func=ACT.Relu)
 
-        def feature(u):
-            if u not in ON_G:
+        def feature(u, hs):
+            if u not in ON_G and u not in ON_S:
                 return
-            f = work.tile([P, S, P], F32, name="f", tag="f", bufs=2, align_bytes=64)
-            ht[u] = f
-            for h in range(2):
+            if 0 in hs:
+                f = work.tile([P, S, P], F32, name="f", tag="f", bufs=4, align_bytes=64)
+                ht[u] = f
+            f = ht[u]
+            for h in hs:
                 nc.scalar.activation(
                     out=f[:, :, HS * h : HS * h + HS],
                     in_=vt[u, h][:].rearrange("p (i j) -> p j i", j=S),
@@ -281,27 +336,32 @@ def tile_attentive_set_pool_f2_kernel(
 
         def take(u):
             f = u % 4
-            if u // 4 in LN:
+            q = u // 4
+            if q in LN or q == 3:
                 if f == 3:
-                    q = u // 4
                     r = work.tile([P, 4, P], F32, name="rq", tag="rq", bufs=2, align_bytes=64)
                     rt[q] = r
-                    nc.scalar.activation(out=r[:], in_=Et[q][:].rearrange("s (p t) -> s t p", t=4), func=ACT.Ln)
-                    nc.scalar.activation(out=r[:], in_=r[:], func=ACT.Exp, scale=-1.0)
+                    total = Et[q][:].rearrange("s (p t) -> s t p", t=4)
+                    if q == 3:
+                        nc.scalar.activation(out=r[:], in_=total, func=ACT.Abs_reciprocal_sqrt)
+                        nc.scalar.activation(out=r[:], in_=r[:], func=ACT.Square)
+                    else:
+                        nc.scalar.activation(out=r[:], in_=total, func=ACT.Ln)
+                        nc.scalar.activation(out=r[:], in_=r[:], func=ACT.Exp, scale=-1.0)
                 return
             r = work.tile([P, 4, 32], F32, name="r", tag="r", bufs=4, align_bytes=64)
             rt["u", u] = r
             nc.scalar.copy(out=r[:], in_=Et[u // 4][:, P * f : P * f + P].rearrange("s (p t) -> s t p", t=4))
 
         def inv_u(u):
-            if u // 4 in LN:
+            if u // 4 in LN or u // 4 == 3:
                 return
             r = rt["u", u]
             nc.vector.reciprocal(out=r[:], in_=r[:])
 
         def div_u(u):
             f, q = u % 4, u // 4
-            if q in LN:
+            if q in LN or q == 3:
                 if f == 3:
                     new_po(q)
                     nc.vector.tensor_tensor(
@@ -339,9 +399,12 @@ def tile_attentive_set_pool_f2_kernel(
 
         yt, sst, zt, rst = {}, {}, {}, {}
 
-        def project(st, nt, tag, bufs):
-            acc = bank(tag, bufs)
-            for g in range(G):
+        def project(st, nt, gs, tag, bufs):
+            if 0 in gs:
+                acc = bank(tag, bufs)
+                zt[st, nt] = acc
+            acc = zt[st, nt]
+            for g in gs:
                 q = 2 * st + g
                 nc.tensor.matmul_mx(
                     out=acc[:],
@@ -352,7 +415,6 @@ def tile_attentive_set_pool_f2_kernel(
                     start=(g == 0),
                     stop=(g == G - 1),
                 )
-            zt[st, nt] = acc
 
         def shift(st, nt):
             if nt == 0:
@@ -367,16 +429,19 @@ def tile_attentive_set_pool_f2_kernel(
             nc.scalar.activation(out=sq[:], in_=yt[st, nt][:], func=ACT.Square, accum_out=sst[st][:, nt : nt + 1])
 
         def norm(st):
-            ms = work.tile([P, 1], F32, name="ms", tag="ms", bufs=2, align_bytes=64)
+            tot = work.tile([P, 1], F32, name="tot", tag="tot", bufs=2, align_bytes=64)
             rs = work.tile([P, 1], F32, name="rs", tag="rs", bufs=2, align_bytes=64)
+            sc = work.tile([P, 4], F32, name="sc", tag="sc", bufs=2, align_bytes=64)
             rst[st] = rs
-            nc.vector.tensor_reduce(out=ms[:], in_=sst[st][:], axis=AX.X, op=ALU.add)
-            nc.vector.tensor_scalar(out=ms[:], in0=ms[:], scalar1=1.0 / D, scalar2=None, op0=ALU.mult)
-            nc.gpsimd.tensor_tensor(out=rs[:], in0=ms[:], in1=neghalf[:], op=ALU.pow)
+            nc.scalar.activation(out=sc[:], in_=sst[st][:], func=ACT.Identity, scale=1.0 / D, accum_out=tot[:])
+            if st == 0:
+                nc.gpsimd.tensor_tensor(out=rs[:], in0=tot[:], in1=neghalf[:], op=ALU.pow)
+            else:
+                nc.scalar.activation(out=rs[:], in_=tot[:], func=ACT.Abs_reciprocal_sqrt)
 
         def gain(st, nt, eng):
             y = yt[st, nt]
-            yg = work.tile([P, BANK], F32, name="yg", tag="yg", bufs=4, align_bytes=64)
+            yg = work.tile([P, BANK], F32, name="yg", tag="yg", bufs=8, align_bytes=64)
             yt[st, nt] = yg
             eng.tensor_tensor(out=yg[:], in0=y[:], in1=gb[:, BANK * nt : BANK * nt + BANK], op=ALU.mult)
 
@@ -393,9 +458,8 @@ def tile_attentive_set_pool_f2_kernel(
 
         def finish(st, nt):
             y = yt[st, nt]
-            nc.vector.scalar_tensor_tensor(
-                out=y[:], in0=y[:], scalar=rst[st][:], in1=gb[:, BANK * nt : BANK * nt + BANK], op0=ALU.mult, op1=ALU.mult
-            )
+            nc.scalar.activation(out=y[:], in_=y[:], func=ACT.Copy, scale=rst[st][:])
+            gain(st, nt, nc.gpsimd)
             store(st, nt)
 
         stage = {
@@ -408,6 +472,7 @@ def tile_attentive_set_pool_f2_kernel(
             "mx_v": mx_v,
             "add_prior": add_prior,
             "weight_v": weight_v,
+            "weight_s": weight_s,
             "maximum": maximum,
             "weight_g": weight_g,
             "subtract": subtract,
@@ -421,22 +486,26 @@ def tile_attentive_set_pool_f2_kernel(
             "quant": quant,
         }
         proj_stage = {
-            "project": lambda nt: project(0, nt, "misc", 1),
+            "project": lambda nt: project(0, nt, (0, 1), "misc", 1),
             "shift": lambda nt: shift(0, nt),
             "square": lambda nt: square(0, nt),
         }
 
-        mx_a(0)
-        bp = bank("misc", 1)
-        nc.tensor.matmul(bp[:, 0:FT], lhsT=brow[:], rhs=identb[:, 0:FT], start=True, stop=True)
-        nc.vector.tensor_copy(out=bcol[:], in_=bp[:, 0:FT])
-        last = max(NU - 1 + max(back for name, back in STEP if name in stage), FIN0 + 2)
+        mx_a(0, (0, 1))
+        last = max(NU - 1 + max(entry[1] for entry in STEP if entry[0] in stage), FIN0 + 2)
         for k in range(last + 1):
-            for name, back in STEP:
+            if k == 1:
+                spread_bias()
+            if k == 2 or k == 3:
+                spread_prior(k, "misc", 1, "S")
+            for name, back, hs in STEP:
                 if name in stage:
                     u = k - back
                     if 0 <= u < NU and not (name == "mx_a" and u == 0) and not (name == "div_u" and u == NU - 1):
-                        stage[name](u)
+                        if name in HALVED:
+                            stage[name](u, hs)
+                        else:
+                            stage[name](u)
                 elif name in half_stage:
                     q, rem = divmod(k - back - 3, 4)
                     if rem == 0 and 0 <= q < 3:
@@ -444,6 +513,9 @@ def tile_attentive_set_pool_f2_kernel(
                 else:
                     if 0 <= k - back < 4:
                         proj_stage[name](k - back)
+            for nt in range(4):
+                if k == EP[nt // 2]:
+                    project(1, nt, (0,), "aavv"[nt], BANKS[nt // 2])
             if k == FIN0:
                 norm(0)
             if 0 <= k - FIN0 - 1 < 2 :
@@ -454,7 +526,7 @@ def tile_attentive_set_pool_f2_kernel(
         leave(3, "V")
         quant(3)
         for nt in range(4):
-            project(1, nt, "av"[nt % 2], BANKS[nt % 2])
+            project(1, nt, (1,), "", 0)
         for nt in range(4):
             shift(1, nt)
             square(1, nt)
@@ -463,5 +535,5 @@ def tile_attentive_set_pool_f2_kernel(
         gain(1, 2, nc.vector)
         norm(1)
         gain(1, 3, nc.vector)
-        for nt in (2, 3, 0, 1):
-            scale_out(1, nt, "SV"[nt % 2])
+        for nt in (0, 2, 1, 3):
+            scale_out(1, nt, "VVSV"[nt])

from contextlib import ExitStack

import concourse.mybir as mybir
from concourse.masks import make_identity

F32 = mybir.dt.float32
BF16 = mybir.dt.bfloat16
U32 = mybir.dt.uint32
I32 = mybir.dt.int32
U8 = mybir.dt.uint8
FP4 = mybir.dt.float4_e2m1fn_x4
FP8 = mybir.dt.float8_e4m3fn_x4
ALU = mybir.AluOpType
ACT = mybir.ActivationFunctionType
AX = mybir.AxisListType

P = 128
B, S, K, F, D = 256, 8, 1024, 1024, 2048
NM = B * S
G = 2
FT = 8
NU = 2 * FT
HS = 64
BANK = 512

FLOPS = 2 * 2 * NM * K * F + 2 * B * F * D

SPLIT = (0, 1, 15)

ON_G = (10, 13)
ON_S = (2, 6, 14, 15)
STEP = (
    ("square", 22, (0, 1)),
    ("mx_v", 2, (0, 1)),
    ("add_prior", 0, (0,)),
    ("mx_a", -1, (0,)),
    ("feature", 3, (1,)),
    ("relu", 4, (0, 1)),
    ("weight_v", 3, (1,)),
    ("add_prior", 0, (1,)),
    ("shift", 15, (0, 1)),
    ("sum_e", 2, (0, 1)),
    ("inv_u", 3, (0, 1)),
    ("turn", 5, (0, 1)),
    ("weight_g", 3, (0, 1)),
    ("feature", 2, (0,)),
    ("weight_v", 2, (0,)),
    ("weight_s", 3, (1,)),
    ("leave", 5, (0, 1)),
    ("sum_g", 4, (0, 1)),
    ("quant", 7, (0, 1)),
    ("maximum", 0, (0,)),
    ("subtract", 0, (0,)),
    ("mx_a", -1, (1,)),
    ("weight_s", 2, (0,)),
    ("maximum", 0, (1,)),
    ("project", 14, (0, 1)),
    ("div_u", 4, (0, 1)),
    ("subtract", 0, (1,)),
    ("exponent", 1, (0, 1)),
    ("take", 2, (0, 1)),
)
FIN0 = 34
BANKS = (2, 3, 1)
LN = (0, 1, 2)
EP = (30, 29)


HALVED = ("mx_a", "mx_v", "add_prior", "maximum", "subtract", "exponent", "weight_v", "weight_s", "feature")


def tile_attentive_set_pool_f2_kernel(
    tc, x_words, x_scales, wv_words, wv_scales, wa_words, wa_scales, b, prior, wo_words, wo_scales, c, gain, out
):
    nc = tc.nc
    with ExitStack() as ctx:
        keep = ctx.enter_context(tc.tile_pool(name="keep", bufs=1))
        work = ctx.enter_context(tc.tile_pool(name="work", bufs=3))
        ps = ctx.enter_context(tc.psum_pool(name="ps", bufs=1))
        ctx.enter_context(tc.manual_schedule())

        def const(shape, dtype, name):
            t = keep.tile(shape, dtype, name=name, tag=name, bufs=1, align_bytes=64)
            return t

        xa, xb, xc = const([P, G, 1024], U8, "xa"), const([P, G, 1024], U8, "xb"), const([P, G, NM], U8, "xc")
        wa_first, wa_rest = const([P, G, 512], U8, "wa0"), const([P, G, 1536], U8, "wa1")
        wv = const([P, G, 2 * F], U8, "wv")
        wo = const([P, G, 2 * D], U8, "wo")
        xs, was = const([P, G * NM], U8, "xs"), const([P, G * F], U8, "was")
        wvs, wos = const([P, G * F], U8, "wvs"), const([P, G * D], U8, "wos")
        prow = [const([P, 2 * BANK], BF16, "prow0"), const([P, 2 * BANK], BF16, "prow1")]
        brow, ones = const([P, P], BF16, "brow"), const([P, P], BF16, "ones")
        ident, identb = const([P, P], F32, "ident"), const([P, P], BF16, "identb")
        pr = const([P, 4, 4, HS, 2], F32, "pr")
        bcol = const([P, FT], F32, "bcol")
        cb, gb = const([P, D], BF16, "cb"), const([P, D], BF16, "gb")
        dummy, neghalf = const([P, 1], F32, "dummy"), const([P, 1], F32, "neghalf")

        nc.vector.memset(was[:].bitcast(I32), 0)
        nc.vector.memset(xs[:].bitcast(I32), 0)
        nc.vector.memset(prow[0][:].bitcast(U32), 0)
        nc.vector.memset(dummy[:], 0.0)
        nc.vector.memset(ones[:], 1.0)
        nc.vector.memset(brow[:].bitcast(U32), 0)
        nc.vector.memset(prow[1][:].bitcast(U32), 0)
        nc.vector.memset(wvs[:].bitcast(I32), 0)
        nc.vector.memset(wos[:].bitcast(I32), 0)
        nc.vector.memset(neghalf[:], -0.5)

        def words(tile, dram, lo, hi):
            nc.sync.dma_start(out=tile[:], in_=dram.rearrange("g p c -> p g c")[:, :, lo:hi])

        def scales(eng, tile, dram, q):
            eng.dma_start(
                out=tile[32 * q : 32 * q + 4, :].bitcast(I32).rearrange("p (g n) -> p g n", g=G),
                in_=dram[:, 4 * q : 4 * q + 4, :].bitcast(I32).rearrange("g q n -> q g n"),
            )

        prior_row = prior.rearrange("(o s) j -> o (s j)", o=1)
        for q in range(4):
            scales(nc.scalar, was, wa_scales, q)
        for q in range(4):
            scales(nc.sync, xs, x_scales, q)
        words(wa_first, wa_words, 0, 512)
        words(xa, x_words, 0, 1024)
        words(xb, x_words, 1024, 2048)
        nc.scalar.dma_start(out=prow[0][0:1, :], in_=prior_row[:, 0 : 2 * BANK])
        nc.scalar.activation(out=dummy[:], in_=dummy[:], func=ACT.Exp)
        make_identity(nc, identb[:])
        make_identity(nc, ident[:])
        nc.gpsimd.dma_start(out=brow[0:FT, :], in_=b.rearrange("(c p) -> c p", c=FT))
        nc.gpsimd.dma_start(out=prow[1][0:1, :], in_=prior_row[:, 2 * BANK : 4 * BANK])
        words(wa_rest, wa_words, 512, 2048)
        for q in range(4):
            scales(nc.sync, wvs, wv_scales, q)
        words(wv, wv_words, 0, 2048)
        words(xc, x_words, 2048, 4096)
        for q in range(4):
            scales(nc.sync, wos, wo_scales, q)
        words(wo, wo_words, 0, 4096)
        nc.sync.dma_start(out=cb[:], in_=c.partition_broadcast(P))
        nc.sync.dma_start(out=gb[:], in_=gain.partition_broadcast(P))

        def bank(tag, bufs):
            t = ps.tile([P, BANK], F32, name=tag, tag=tag, bufs=bufs)
            return t

        def spread_prior(h, tag, bufs, eng):
            pp = bank(tag, bufs)
            n0 = BANK * (h % 2)
            nc.tensor.matmul(pp[:], lhsT=ones[:], rhs=prow[h // 2][:, n0 : n0 + BANK], start=True, stop=True)
            src = pp[:].rearrange("p (i a l) -> p a i l", a=4, l=2)
            if eng == "V":
                nc.vector.tensor_copy(out=pr[:, h], in_=src)
            else:
                nc.scalar.copy(out=pr[:, h], in_=src)

        spread_prior(0, "v", BANKS[1], "V")
        spread_prior(1, "v", BANKS[1], "S")

        def spread_bias():
            bp = bank("misc", 1)
            nc.tensor.matmul(bp[:, 0:FT], lhsT=brow[:], rhs=identb[:, 0:FT], start=True, stop=True)
            nc.scalar.copy(out=bcol[:], in_=bp[:, 0:FT])

        at, vt, lt, mt, dt, et, gt, ht = {}, {}, {}, {}, {}, {}, {}, {}
        Et, Nt, rt, pot = {}, {}, {}, {}
        btt, ptt, codes, cscale = {}, {}, {}, {}

        def members(st, h):
            if st == 0:
                return (xa, xb)[h][:]
            return xc[:, :, 1024 * h : 1024 * h + 1024]

        def mx(u, w, lo, s, h, tag):
            st, ft = divmod(u, FT)
            acc = bank(tag, BANKS[0] if tag == "a" else BANKS[1])
            n0 = BANK * h
            for g in range(G):
                nc.tensor.matmul_mx(
                    out=acc[:],
                    lhsT=w[:, g, 256 * (ft - lo) : 256 * (ft - lo) + 256].bitcast(FP4),
                    lhsT_scale=s[:, F * g + P * ft : F * g + P * ft + P],
                    rhs=members(st, h)[:, g, :].bitcast(FP4),
                    rhs_scale=xs[:, NM * g + 1024 * st + n0 : NM * g + 1024 * st + n0 + BANK],
                    start=(g == 0),
                    stop=(g == G - 1),
                )
            return acc

        def mx_a(u, hs):
            for h in hs:
                if u % FT < 2:
                    at[u, h] = mx(u, wa_first, 0, was, h, "a")
                else:
                    at[u, h] = mx(u, wa_rest, 2, was, h, "a")

        def mx_v(u, hs):
            for h in hs:
                vt[u, h] = mx(u, wv, 0, wvs, h, "v")

        def runs(u, hs):
            if hs == (0, 1) and u not in SPLIT:
                return [(0, P)]
            return [(HS * h, HS * h + HS) for h in hs]

        def new(store, u, hs, shape, name, bufs):
            if 0 in hs:
                t = work.tile(shape, F32, name=name, tag=name, bufs=bufs, align_bytes=64)
                store[u] = t
            return store[u]

        def add_prior(u, hs):
            l = new(lt, u, hs, [P, 4, P, 2], "l", 4)
            for h in hs:
                nc.vector.tensor_tensor(
                    out=l[:, :, HS * h : HS * h + HS, :],
                    in0=at[u, h][:].rearrange("p (i a l) -> p a i l", a=4, l=2),
                    in1=pr[:, 2 * (u // FT) + h],
                    op=ALU.add,
                )

        def maximum(u, hs):
            m = new(mt, u, hs, [P, P], "m", 3)
            for lo, hi in runs(u, hs):
                nc.vector.tensor_reduce(
                    out=m[:, lo:hi], in_=lt[u][:, :, lo:hi, :].rearrange("p a i l -> p i a l"), axis=AX.XY, op=ALU.max
                )

        def subtract(u, hs):
            d = new(dt, u, hs, [P, S, P], "d", 3)
            for lo, hi in runs(u, hs):
                eng = nc.vector if u == NU - 1 and lo > 0 else nc.gpsimd
                eng.tensor_tensor(
                    out=d[:, :, lo:hi].rearrange("p (a l) i -> p a l i", l=2),
                    in0=lt[u][:, :, lo:hi, :].rearrange("p a i l -> p a l i"),
                    in1=mt[u][:, lo:hi].unsqueeze(1).unsqueeze(1).to_broadcast([P, 4, 2, hi - lo]),
                    op=ALU.subtract,
                )

        def exponent(u, hs):
            e = new(et, u, hs, [P, S, P], "e", 5)
            for lo, hi in runs(u, hs):
                nc.scalar.activation(out=e[:, :, lo:hi], in_=dt[u][:, :, lo:hi], func=ACT.Exp)
            if u == NU - 1 and 1 in hs:
                nc.scalar.activation(out=dummy[:], in_=dummy[:], func=ACT.Abs_reciprocal_sqrt)

        def new_g(u):
            g = work.tile([P, S, P], F32, name="g", tag="g", bufs=4, align_bytes=64)
            gt[u] = g
            return g

        def weight_v(u, hs):
            if u in ON_G or u in ON_S:
                return
            if 0 in hs:
                new_g(u)
            g = gt[u]
            for h in hs:
                r = slice(HS * h, HS * h + HS)
                nc.vector.scalar_tensor_tensor(
                    out=g[:, :, r],
                    in0=vt[u, h][:].rearrange("p (i j) -> p j i", j=S),
                    scalar=bcol[:, u % FT : u % FT + 1],
                    in1=et[u][:, :, r],
                    op0=ALU.add,
                    op1=ALU.mult,
                )

        def weight_s(u, hs):
            if u not in ON_S:
                return
            if 0 in hs:
                new_g(u)
            for lo, hi in runs(u, hs):
                nc.vector.tensor_tensor(
                    out=gt[u][:, :, lo:hi], in0=ht[u][:, :, lo:hi], in1=et[u][:, :, lo:hi], op=ALU.mult
                )

        def relu(u):
            if u in ON_G or u in ON_S:
                return
            g = gt[u]
            if u == NU - 1:
                for h in range(2):
                    r = slice(HS * h, HS * h + HS)
                    nc.scalar.activation(out=g[:, :, r], in_=g[:, :, r], func=ACT.Relu)
            else:
                nc.scalar.activation(out=g[:], in_=g[:], func=ACT.Relu)

        def feature(u, hs):
            if u not in ON_G and u not in ON_S:
                return
            if 0 in hs:
                f = work.tile([P, S, P], F32, name="f", tag="f", bufs=4, align_bytes=64)
                ht[u] = f
            f = ht[u]
            for h in hs:
                nc.scalar.activation(
                    out=f[:, :, HS * h : HS * h + HS],
                    in_=vt[u, h][:].rearrange("p (i j) -> p j i", j=S),
                    func=ACT.Relu,
                    bias=bcol[:, u % FT : u % FT + 1],
                )

        def weight_g(u):
            if u not in ON_G:
                return
            g = new_g(u)
            nc.gpsimd.tensor_tensor(out=g[:], in0=ht[u][:], in1=et[u][:], op=ALU.mult)

        def sums(u, src, store, tag, bufs):
            f = u % 4
            if f == 0:
                store[u // 4] = bank(tag, bufs)
            for j in range(S):
                nc.tensor.matmul(
                    store[u // 4][:, P * f : P * f + P],
                    lhsT=src[u][:, j, :],
                    rhs=ident[:],
                    is_transpose=True,
                    start=(j == 0),
                    stop=(j == S - 1),
                )

        def sum_e(u):
            sums(u, et, Et, "E", 1)

        def sum_g(u):
            sums(u, gt, Nt, "N", BANKS[2])

        def new_po(q):
            po = work.tile([P, 4, P], BF16, name="po", tag="po", bufs=2, align_bytes=64)
            pot[q] = po

        def take(u):
            f = u % 4
            q = u // 4
            if q in LN or q == 3:
                if f == 3:
                    r = work.tile([P, 4, P], F32, name="rq", tag="rq", bufs=2, align_bytes=64)
                    rt[q] = r
                    total = Et[q][:].rearrange("s (p t) -> s t p", t=4)
                    if q == 3:
                        nc.scalar.activation(out=r[:], in_=total, func=ACT.Abs_reciprocal_sqrt)
                        nc.scalar.activation(out=r[:], in_=r[:], func=ACT.Square)
                    else:
                        nc.scalar.activation(out=r[:], in_=total, func=ACT.Ln)
                        nc.scalar.activation(out=r[:], in_=r[:], func=ACT.Exp, scale=-1.0)
                return
            r = work.tile([P, 4, 32], F32, name="r", tag="r", bufs=4, align_bytes=64)
            rt["u", u] = r
            nc.scalar.copy(out=r[:], in_=Et[u // 4][:, P * f : P * f + P].rearrange("s (p t) -> s t p", t=4))

        def inv_u(u):
            if u // 4 in LN or u // 4 == 3:
                return
            r = rt["u", u]
            nc.vector.reciprocal(out=r[:], in_=r[:])

        def div_u(u):
            f, q = u % 4, u // 4
            if q in LN or q == 3:
                if f == 3:
                    new_po(q)
                    nc.vector.tensor_tensor(
                        out=pot[q][:], in0=Nt[q][:].rearrange("s (p t) -> s t p", t=4), in1=rt[q][:], op=ALU.mult
                    )
                return
            if f == 0:
                new_po(q)
            nc.vector.tensor_tensor(
                out=pot[q][:, :, 32 * f : 32 * f + 32],
                in0=Nt[q][:, P * f : P * f + P].rearrange("s (p t) -> s t p", t=4),
                in1=rt["u", u][:],
                op=ALU.mult,
            )

        def turn(q):
            bt = ps.tile([P, 4, P], BF16, name="bt", tag="misc", bufs=1)
            btt[q] = bt
            for t in range(4):
                nc.tensor.transpose(bt[:, t, :], pot[q][:, t, :], identb[:])

        def leave(q, eng):
            pt = work.tile([P, P, 4], BF16, name="pt", tag="pt", bufs=2, align_bytes=64)
            ptt[q] = pt
            if eng == "S":
                nc.scalar.copy(out=pt[:], in_=btt[q][:].rearrange("p t n -> p n t"))
            else:
                nc.vector.tensor_copy(out=pt[:], in_=btt[q][:].rearrange("p t n -> p n t"))

        def quant(q):
            cd = work.tile([P, P], U32, name="cd", tag="cd", bufs=4, align_bytes=64)
            cs = work.tile([P, P], U8, name="cs", tag="cs", bufs=4, align_bytes=64)
            nc.vector.quantize_mx(out=cd[:].bitcast(FP8), scales=cs[:], in_=ptt[q][:].rearrange("p n t -> p (n t)"))
            codes[q], cscale[q] = cd, cs

        yt, sst, zt, rst = {}, {}, {}, {}

        def project(st, nt, gs, tag, bufs):
            if 0 in gs:
                acc = bank(tag, bufs)
                zt[st, nt] = acc
            acc = zt[st, nt]
            for g in gs:
                q = 2 * st + g
                nc.tensor.matmul_mx(
                    out=acc[:],
                    lhsT=codes[q][:].bitcast(FP8),
                    lhsT_scale=cscale[q][:],
                    rhs=wo[:, g, 1024 * nt : 1024 * nt + 1024].bitcast(FP4),
                    rhs_scale=wos[:, D * g + BANK * nt : D * g + BANK * nt + BANK],
                    start=(g == 0),
                    stop=(g == G - 1),
                )

        def shift(st, nt):
            if nt == 0:
                ss = work.tile([P, 4], F32, name="ss", tag="ss", bufs=2, align_bytes=64)
                sst[st] = ss
            y = work.tile([P, BANK], F32, name="y", tag="y", bufs=8, align_bytes=64)
            yt[st, nt] = y
            nc.vector.tensor_tensor(out=y[:], in0=zt[st, nt][:], in1=cb[:, BANK * nt : BANK * nt + BANK], op=ALU.add)

        def square(st, nt):
            sq = work.tile([P, BANK], BF16, name="sq", tag="sq", bufs=2, align_bytes=64)
            nc.scalar.activation(out=sq[:], in_=yt[st, nt][:], func=ACT.Square, accum_out=sst[st][:, nt : nt + 1])

        def norm(st):
            tot = work.tile([P, 1], F32, name="tot", tag="tot", bufs=2, align_bytes=64)
            rs = work.tile([P, 1], F32, name="rs", tag="rs", bufs=2, align_bytes=64)
            sc = work.tile([P, 4], F32, name="sc", tag="sc", bufs=2, align_bytes=64)
            rst[st] = rs
            nc.scalar.activation(out=sc[:], in_=sst[st][:], func=ACT.Identity, scale=1.0 / D, accum_out=tot[:])
            if st == 0:
                nc.gpsimd.tensor_tensor(out=rs[:], in0=tot[:], in1=neghalf[:], op=ALU.pow)
            else:
                nc.scalar.activation(out=rs[:], in_=tot[:], func=ACT.Abs_reciprocal_sqrt)

        def gain(st, nt, eng):
            y = yt[st, nt]
            yg = work.tile([P, BANK], F32, name="yg", tag="yg", bufs=8, align_bytes=64)
            yt[st, nt] = yg
            eng.tensor_tensor(out=yg[:], in0=y[:], in1=gb[:, BANK * nt : BANK * nt + BANK], op=ALU.mult)

        def store(st, nt):
            nc.sync.dma_start(out=out[P * st : P * st + P, BANK * nt : BANK * nt + BANK], in_=yt[st, nt][:])

        def scale_out(st, nt, eng):
            y = yt[st, nt]
            if eng == "S":
                nc.scalar.activation(out=y[:], in_=y[:], func=ACT.Copy, scale=rst[st][:])
            else:
                nc.vector.tensor_scalar(out=y[:], in0=y[:], scalar1=rst[st][:], scalar2=None, op0=ALU.mult)
            store(st, nt)

        def finish(st, nt):
            y = yt[st, nt]
            nc.scalar.activation(out=y[:], in_=y[:], func=ACT.Copy, scale=rst[st][:])
            gain(st, nt, nc.gpsimd)
            store(st, nt)

        stage = {
            "sum_e": sum_e,
            "take": take,
            "inv_u": inv_u,
            "div_u": div_u,
            "sum_g": sum_g,
            "mx_a": mx_a,
            "mx_v": mx_v,
            "add_prior": add_prior,
            "weight_v": weight_v,
            "weight_s": weight_s,
            "maximum": maximum,
            "weight_g": weight_g,
            "subtract": subtract,
            "feature": feature,
            "exponent": exponent,
            "relu": relu,
        }
        half_stage = {
            "turn": turn,
            "leave": lambda q: leave(q, "S"),
            "quant": quant,
        }
        proj_stage = {
            "project": lambda nt: project(0, nt, (0, 1), "misc", 1),
            "shift": lambda nt: shift(0, nt),
            "square": lambda nt: square(0, nt),
        }

        mx_a(0, (0, 1))
        last = max(NU - 1 + max(entry[1] for entry in STEP if entry[0] in stage), FIN0 + 2)
        for k in range(last + 1):
            if k == 1:
                spread_bias()
            if k == 2 or k == 3:
                spread_prior(k, "misc", 1, "S")
            for name, back, hs in STEP:
                if name in stage:
                    u = k - back
                    if 0 <= u < NU and not (name == "mx_a" and u == 0) and not (name == "div_u" and u == NU - 1):
                        if name in HALVED:
                            stage[name](u, hs)
                        else:
                            stage[name](u)
                elif name in half_stage:
                    q, rem = divmod(k - back - 3, 4)
                    if rem == 0 and 0 <= q < 3:
                        half_stage[name](q)
                else:
                    if 0 <= k - back < 4:
                        proj_stage[name](k - back)
            for nt in range(4):
                if k == EP[nt // 2]:
                    project(1, nt, (0,), "aavv"[nt], BANKS[nt // 2])
            if k == FIN0:
                norm(0)
            if 0 <= k - FIN0 - 1 < 2 :
                finish(0, 2 * (k - FIN0 - 1))
                finish(0, 2 * (k - FIN0 - 1) + 1)
        div_u(NU - 1)
        turn(3)
        leave(3, "V")
        quant(3)
        for nt in range(4):
            project(1, nt, (1,), "", 0)
        for nt in range(4):
            shift(1, nt)
            square(1, nt)
            if nt < 2:
                gain(1, nt, nc.gpsimd)
        gain(1, 2, nc.vector)
        norm(1)
        gain(1, 3, nc.vector)
        for nt in (0, 2, 1, 3):
            scale_out(1, nt, "VVSV"[nt])
